import numpy as np
import ml_dtypes


def mxq(x, axis, fmt="e4m3"):
    dtype, down = {"e4m3": (ml_dtypes.float8_e4m3fn, 7), "e5m2": (ml_dtypes.float8_e5m2, 14)}[fmt]
    v = np.moveaxis(np.asarray(x, np.float32).astype(ml_dtypes.bfloat16).astype(np.float64), axis, -1)
    blocks = v.reshape(v.shape[:-1] + (-1, 32))
    amax = np.abs(blocks).max(-1, keepdims=True)
    byte = np.maximum(np.where(amax > 0, np.frexp(amax)[1] - 1 + 127, 0) - down, 1)
    scale = np.exp2(byte - 127.0)
    codes = (blocks / scale).astype(np.float32).astype(dtype).astype(np.float64)
    return np.moveaxis((codes * scale).reshape(v.shape), -1, axis)


WIDE = False


def mx_kscale(k):
    if not WIDE:
        return np.ones(k)
    levels = np.array([10, -10, 5, -5, 0])
    if k % 512:
        return np.exp2(np.random.permutation(np.resize(levels, k // 32))).repeat(32)
    a = np.empty((k // 512, 16))
    for p in range(k // 512):
        a[p, :8] = np.random.permutation(np.resize(levels, 8))
        for g in range(8):
            far = levels[np.abs(levels - a[p, g]) >= 10]
            a[p, g + 8] = far[np.random.randint(len(far))]
    return np.exp2(a.ravel()).repeat(32)


def f64(x):
    return np.asarray(x).astype(np.float64)


def striped(idx):
    return np.tile(idx.reshape(-1, 16).T, (8, 1)).astype(np.uint16)


def unstriped(offs):
    return offs[:16].T.reshape(-1).astype(np.int64)


E2M1 = np.array([0.0, 0.5, 1.0, 1.5, 2.0, 3.0, 4.0, 6.0, -0.0, -0.5, -1.0, -1.5, -2.0, -3.0, -4.0, -6.0])


def pack_weight(w, fmt):
    k, n = w.shape
    w = f64(np.asarray(w, np.float32).astype(ml_dtypes.bfloat16)).reshape(k // 32, 32, n)
    amax = np.abs(w).max(1)
    if fmt == "e4m3":
        byte = np.frexp(amax)[1] - 1 + 127 - 7
    else:
        mant, ex = np.frexp(amax / 6.0)
        byte = np.where(mant > 0.5, ex, ex - 1) + 127
    byte = np.clip(np.where(amax > 0, byte, 1), 1, 254)
    scaled = (w * np.exp2(127.0 - byte)[:, None, :]).reshape(k, n).astype(np.float32)
    by_word = np.ascontiguousarray(scaled.reshape(k // 512, 128, 4, n).transpose(0, 1, 3, 2))
    if fmt == "e4m3":
        words = by_word.astype(ml_dtypes.float8_e4m3fn).view(np.uint8)
    else:
        c = by_word.astype(ml_dtypes.float4_e2m1fn).view(np.uint8) & 0xF
        words = (c[..., 0::2] | (c[..., 1::2] << 4)).reshape(k // 512, 128, 2 * n)
    return np.ascontiguousarray(words), np.ascontiguousarray(byte.astype(np.uint8).reshape(k // 512, 16, n))


def unpack_weight(words, scales, fmt):
    g, _, n = scales.shape
    words = np.ascontiguousarray(words).reshape(g, 128, n, -1)
    if fmt == "e4m3":
        vals = words.view(ml_dtypes.float8_e4m3fn).astype(np.float64)
    else:
        nib = np.empty((g, 128, n, 4), np.uint8)
        nib[..., 0::2] = words & 0xF
        nib[..., 1::2] = words >> 4
        vals = E2M1[nib]
    vals = vals * np.repeat(np.exp2(scales.astype(np.float64) - 127.0), 8, axis=1)[..., None]
    return vals.transpose(0, 1, 3, 2).reshape(g * 512, n)


K, T, E, C, N = 1024, 512, 2, 256, 512
K8 = 512


def by_expert(wq, xq):
    return np.concatenate([wq[e].T @ xq[:, e * C:(e + 1) * C] for e in range(E)], axis=1)


def setup_inputs():
    n = np.random.standard_normal
    s = mx_kscale(K)[:, None]
    w = n((E, K, N)) / np.sqrt(K) / s[None]
    w8 = [pack_weight(m[:K8], "e4m3") for m in w]
    w4 = [pack_weight(m[K8:], "e2m1") for m in w]
    return {
        "xT": (n((K, T)) * s).astype(np.float32),
        "w8_words": np.stack([m[0] for m in w8]),
        "w8_scales": np.stack([m[1] for m in w8]),
        "w4_words": np.stack([m[0] for m in w4]),
        "w4_scales": np.stack([m[1] for m in w4]),
        "b": (0.3 * n((N, E))).astype(np.float32),
        "gate": np.tile(np.random.uniform(0.2, 1.0, E * C), (N, 1)).astype(np.float32),
        "offs": striped(np.random.permutation(T)[:E * C]),
        "dst": striped(np.random.permutation(T)[:E * C]),
    }


def reference(xT, w8_words, w8_scales, w4_words, w4_scales, b, gate, offs, dst):
    idx = unstriped(offs)
    w = np.stack([np.concatenate([unpack_weight(w8_words[e], w8_scales[e], "e4m3"), unpack_weight(w4_words[e], w4_scales[e], "e2m1")]) for e in range(E)])
    xq = mxq(f64(xT)[:, idx], 0, "e4m3")
    y = by_expert(w, xq)
    y = y + np.repeat(f64(b), C, axis=1)
    out = np.zeros((N, T))
    out[:, unstriped(dst)] = f64(gate) * y
    return out

@@ -1,0 +1,135 @@
+import concourse.mybir as mybir
+
+F32 = mybir.dt.float32
+BF16 = mybir.dt.bfloat16
+U32 = mybir.dt.uint32
+I32 = mybir.dt.int32
+U16 = mybir.dt.uint16
+U8 = mybir.dt.uint8
+FP8X4 = mybir.dt.float8_e4m3fn_x4
+FP4X4 = mybir.dt.float4_e2m1fn_x4
+IDENTITY = mybir.ActivationFunctionType.Identity
+MULT = mybir.AluOpType.mult
+
+P = 128
+K, T, E, C, N = 1024, 512, 2, 256, 512
+PASSES = 2
+PACK = 4
+K_PASS = P * PACK
+N_TILES = N // P
+FLOPS = 2 * K * E * C * N
+BYTES = 4 * K * T + E * 512 * N + E * 256 * N + 2 * E * 16 * N + 4 * N * E + 4 * E * C + 4 * E * C + 4 * N * T
+
+CHUNK = 256
+SCALAR_TOKENS = 80
+
+
+def tile_moe_two_lin_bias_kernel(
+    tc, xT, w8_words, w8_scales, w4_words, w4_scales, b, gate, offs, dst, out
+):
+    nc = tc.nc
+    with (
+        tc.tile_pool(name="held", bufs=1) as held,
+        tc.tile_pool(name="stage", bufs=4) as stage,
+        tc.tile_pool(name="results", bufs=8) as results,
+        tc.psum_pool(name="psum", bufs=8) as psum,
+    ):
+        gather_list = held.tile([P, E * C // 16], U16, name="gather_list")
+        scatter_list = held.tile([P, E * C // 16], U16, name="scatter_list")
+        nc.sync.dma_start(gather_list[:], offs)
+
+        raw = {}
+        for g in range(PASSES):
+            rows = xT[g * K_PASS : (g + 1) * K_PASS, :].rearrange("(p j) w -> p j w", j=PACK)
+            for c in range(0, T, CHUNK):
+                raw[g, c] = stage.tile([P, PACK, CHUNK], F32, name="raw")
+                nc.sync.dma_start(raw[g, c][:], rows[:, :, c : c + CHUNK])
+
+        w_bytes = held.tile([P, 2, E, N], U8, name="w_bytes", align_bytes=64)
+        nc.vector.memset(w_bytes[:].rearrange("p f e n -> p (f e n)").bitcast(I32), 0)
+        tok_bytes = held.tile([P, T], U8, name="tok_bytes", align_bytes=64)
+        nc.gpsimd.memset(tok_bytes[:], 0)
+        for f, scales in ((0, w8_scales), (1, w4_scales)):
+            for r in range(4):
+                nc.sync.dma_start(
+                    w_bytes[32 * r : 32 * r + 4, f].bitcast(I32),
+                    scales[:, 0, 4 * r : 4 * r + 4, :].rearrange("e q n -> q e n").bitcast(I32),
+                )
+        w8 = {}
+        w4 = {}
+        for e in range(E):
+            w8[e] = held.tile([P, 4 * N], U8, name=f"w8_{e}", align_bytes=64)
+            w4[e] = held.tile([P, 2 * N], U8, name=f"w4_{e}", align_bytes=64)
+            nc.sync.dma_start(
+                w8[e][:].bitcast(I32), w8_words[e, 0].rearrange("p n r -> p (n r)").bitcast(I32)
+            )
+            nc.sync.dma_start(w4[e][:].bitcast(I32), w4_words[e, 0].bitcast(I32))
+        bias = held.tile([P, N_TILES, E], F32, name="bias")
+        nc.gpsimd.dma_start(bias[:], b.rearrange("(t p) e -> p t e", p=P))
+        gates = held.tile([P, E * C], F32, name="gates")
+        nc.sync.dma_start(gates[:], gate[0:P, :])
+        nc.sync.dma_start(scatter_list[:], dst)
+
+        tok_words = [held.tile([P, T], U32, name=f"tok_words_{g}", align_bytes=64) for g in range(PASSES)]
+        slot_words = {}
+        slot_bytes = {}
+        first_row = [4, 0]
+
+        for g in range(PASSES):
+            for c in range(0, T, CHUNK):
+                grouped = stage.tile([P, CHUNK, PACK], BF16, name="grouped", align_bytes=64)
+                by_token = raw[g, c][:].rearrange("p j w -> p w j")
+                nc.vector.tensor_copy(grouped[:, SCALAR_TOKENS:, :], by_token[:, SCALAR_TOKENS:, :])
+                nc.scalar.copy(grouped[:, :SCALAR_TOKENS, :], by_token[:, :SCALAR_TOKENS, :])
+                nc.vector.quantize_mx(
+                    out=tok_words[g][:, c : c + CHUNK].bitcast(FP8X4),
+                    scales=tok_bytes[first_row[g] :, c : c + CHUNK],
+                    in_=grouped[:].rearrange("p w j -> p (w j)"),
+                )
+            if g == 0:
+                for e in range(E):
+                    slot_words[g, e] = held.tile([P, C], U32, name=f"slot_words_{g}_{e}", align_bytes=64)
+                    nc.vector.tensor_copy(
+                        slot_words[g, e][:],
+                        tok_words[g][:].indirect(gather_list[:, e * (C // 16) : (e + 1) * (C // 16)]),
+                    )
+
+        def scatter_results(t, y):
+            placed = results.tile([P, T], F32, name="placed")
+            for e in range(E):
+                list_e = scatter_list[:, e * (C // 16) : (e + 1) * (C // 16)]
+                nc.vector.tensor_tensor(placed[:].indirect(list_e), y[t, e][:], gates[:, e * C : (e + 1) * C], MULT)
+            nc.sync.dma_start(out[t * P : (t + 1) * P, :], placed[:])
+
+        y = {}
+        for e in range(E):
+            list_e = gather_list[:, e * (C // 16) : (e + 1) * (C // 16)]
+            slot_words[1, e] = held.tile([P, C], U32, name=f"slot_words_1_{e}", align_bytes=64)
+            slot_bytes[e] = held.tile([P, C], U8, name=f"slot_bytes_{e}", align_bytes=64)
+            nc.vector.tensor_copy(slot_words[1, e][:], tok_words[1][:].indirect(list_e))
+            nc.vector.tensor_copy(slot_bytes[e][:], tok_bytes[:].indirect(list_e))
+            for t in range(N_TILES):
+                acc = psum.tile([P, T], F32, name="acc")
+                for s in range(0, C, P):
+                    nc.tensor.matmul_mx(
+                        out=acc[:, s : s + P],
+                        lhsT=w8[e][:, 4 * P * t : 4 * P * (t + 1)].bitcast(FP8X4),
+                        lhsT_scale=w_bytes[:, 0, e, P * t : P * (t + 1)],
+                        rhs=slot_words[0, e][:, s : s + P].bitcast(FP8X4),
+                        rhs_scale=slot_bytes[e][4:, s : s + P],
+                        start=True,
+                        stop=False,
+                    )
+                    nc.tensor.matmul_mx(
+                        out=acc[:, s : s + P],
+                        lhsT=w4[e][:, 2 * P * t : 2 * P * (t + 1)].bitcast(FP4X4),
+                        lhsT_scale=w_bytes[:, 1, e, P * t : P * (t + 1)],
+                        rhs=slot_words[1, e][:, s : s + P].bitcast(FP8X4),
+                        rhs_scale=slot_bytes[e][:, s : s + P],
+                        start=False,
+                        stop=True,
+                    )
+                y[t, e] = results.tile([P, C], F32, name="y")
+                nc.scalar.activation(y[t, e][:], acc[:, :C], IDENTITY, bias=bias[:, t, e : e + 1])
+        for t in range(N_TILES):
+            scatter_results(t, y)

@@ -1,4 +1,5 @@
 import concourse.mybir as mybir
+from concourse.masks import make_identity
 
 F32 = mybir.dt.float32
 BF16 = mybir.dt.bfloat16
@@ -20,8 +21,7 @@ N_TILES = N // P
 FLOPS = 2 * K * E * C * N
 BYTES = 4 * K * T + E * 512 * N + E * 256 * N + 2 * E * 16 * N + 4 * N * E + 4 * E * C + 4 * E * C + 4 * N * T
 
-CHUNK = 256
-SCALAR_TOKENS = 80
+CHUNKS = ((0, 0, 256, 128), (0, 256, 256, 128), (1, 0, 256, 128), (1, 256, 256, 76))
 
 
 def tile_moe_two_lin_bias_kernel(
@@ -30,91 +30,115 @@ def tile_moe_two_lin_bias_kernel(
     nc = tc.nc
     with (
         tc.tile_pool(name="held", bufs=1) as held,
-        tc.tile_pool(name="stage", bufs=4) as stage,
         tc.tile_pool(name="results", bufs=8) as results,
-        tc.psum_pool(name="psum", bufs=8) as psum,
+        tc.psum_pool(name="psum", bufs=1) as psum,
     ):
         gather_list = held.tile([P, E * C // 16], U16, name="gather_list")
         scatter_list = held.tile([P, E * C // 16], U16, name="scatter_list")
-        nc.sync.dma_start(gather_list[:], offs)
-
-        raw = {}
-        for g in range(PASSES):
-            rows = xT[g * K_PASS : (g + 1) * K_PASS, :].rearrange("(p j) w -> p j w", j=PACK)
-            for c in range(0, T, CHUNK):
-                raw[g, c] = stage.tile([P, PACK, CHUNK], F32, name="raw")
-                nc.sync.dma_start(raw[g, c][:], rows[:, :, c : c + CHUNK])
-
-        w_bytes = held.tile([P, 2, E, N], U8, name="w_bytes", align_bytes=64)
-        nc.vector.memset(w_bytes[:].rearrange("p f e n -> p (f e n)").bitcast(I32), 0)
+        w_bytes = [held.tile([P, E, N], U8, name=f"w_bytes_{f}", align_bytes=64) for f in range(2)]
         tok_bytes = held.tile([P, T], U8, name="tok_bytes", align_bytes=64)
-        nc.gpsimd.memset(tok_bytes[:], 0)
-        for f, scales in ((0, w8_scales), (1, w4_scales)):
-            for r in range(4):
-                nc.sync.dma_start(
-                    w_bytes[32 * r : 32 * r + 4, f].bitcast(I32),
-                    scales[:, 0, 4 * r : 4 * r + 4, :].rearrange("e q n -> q e n").bitcast(I32),
-                )
-        w8 = {}
-        w4 = {}
-        for e in range(E):
-            w8[e] = held.tile([P, 4 * N], U8, name=f"w8_{e}", align_bytes=64)
-            w4[e] = held.tile([P, 2 * N], U8, name=f"w4_{e}", align_bytes=64)
-            nc.sync.dma_start(
-                w8[e][:].bitcast(I32), w8_words[e, 0].rearrange("p n r -> p (n r)").bitcast(I32)
-            )
-            nc.sync.dma_start(w4[e][:].bitcast(I32), w4_words[e, 0].bitcast(I32))
-        bias = held.tile([P, N_TILES, E], F32, name="bias")
-        nc.gpsimd.dma_start(bias[:], b.rearrange("(t p) e -> p t e", p=P))
+        w8 = held.tile([P, E, 4 * N], U8, name="w8", align_bytes=64)
+        w4 = held.tile([P, E, 2 * N], U8, name="w4", align_bytes=64)
+        bias = held.tile([P, E, N_TILES], F32, name="bias")
+        b_rows = held.tile([P, P, E], F32, name="b_rows")
+        identity = held.tile([P, P], F32, name="identity")
         gates = held.tile([P, E * C], F32, name="gates")
+        raw = [held.tile([P, PACK, T], F32, name=f"raw_{g}") for g in range(PASSES)]
+        tok_words = [held.tile([P, T], U32, name=f"tok_words_{g}", align_bytes=64) for g in range(PASSES)]
+
+        for f in range(2):
+            nc.vector.memset(w_bytes[f][:].rearrange("p e n -> p (e n)").bitcast(I32), 0)
+        nc.vector.memset(tok_bytes[:].bitcast(I32), 0)
+
+        def load_tokens(g, c):
+            rows = xT[g * K_PASS : (g + 1) * K_PASS, :].rearrange("(p j) w -> p j w", j=PACK)
+            nc.sync.dma_start(raw[g][:, :, c : c + 256], rows[:, :, c : c + 256])
+
+        def load_scales(f, r):
+            scales = (w8_scales, w4_scales)[f]
+            nc.sync.dma_start(
+                w_bytes[f][32 * r : 32 * r + 4].bitcast(I32),
+                scales[:, 0, 4 * r : 4 * r + 4, :].rearrange("e q n -> q e n").bitcast(I32),
+            )
+
+        nc.gpsimd.memset(b_rows[:], 0.0)
+        nc.scalar.dma_start(b_rows[0:N_TILES], b.rearrange("(t p) e -> t p e", p=P))
+        make_identity(nc, identity[:])
+        load_tokens(0, 0)
+        nc.sync.dma_start(gather_list[:], offs)
+        load_scales(0, 0)
+        load_scales(0, 1)
+        load_tokens(0, 256)
+        load_tokens(1, 0)
+        load_tokens(1, 256)
+        load_scales(0, 2)
+        load_scales(0, 3)
+        for r in range(4):
+            load_scales(1, r)
+        nc.sync.dma_start(w8[:].bitcast(I32), w8_words[:, 0].rearrange("e p n r -> p e (n r)").bitcast(I32))
+        nc.sync.dma_start(w4[:].bitcast(I32), w4_words[:, 0].rearrange("e p n -> p e n").bitcast(I32))
         nc.sync.dma_start(gates[:], gate[0:P, :])
         nc.sync.dma_start(scatter_list[:], dst)
 
-        tok_words = [held.tile([P, T], U32, name=f"tok_words_{g}", align_bytes=64) for g in range(PASSES)]
         slot_words = {}
         slot_bytes = {}
         first_row = [4, 0]
 
-        for g in range(PASSES):
-            for c in range(0, T, CHUNK):
-                grouped = stage.tile([P, CHUNK, PACK], BF16, name="grouped", align_bytes=64)
-                by_token = raw[g, c][:].rearrange("p j w -> p w j")
-                nc.vector.tensor_copy(grouped[:, SCALAR_TOKENS:, :], by_token[:, SCALAR_TOKENS:, :])
-                nc.scalar.copy(grouped[:, :SCALAR_TOKENS, :], by_token[:, :SCALAR_TOKENS, :])
-                nc.vector.quantize_mx(
-                    out=tok_words[g][:, c : c + CHUNK].bitcast(FP8X4),
-                    scales=tok_bytes[first_row[g] :, c : c + CHUNK],
-                    in_=grouped[:].rearrange("p w j -> p (w j)"),
-                )
-            if g == 0:
-                for e in range(E):
-                    slot_words[g, e] = held.tile([P, C], U32, name=f"slot_words_{g}_{e}", align_bytes=64)
-                    nc.vector.tensor_copy(
-                        slot_words[g, e][:],
-                        tok_words[g][:].indirect(gather_list[:, e * (C // 16) : (e + 1) * (C // 16)]),
-                    )
+        def gather_words(g, e):
+            slot_words[g, e] = held.tile([P, C], U32, name=f"slot_words_{g}_{e}", align_bytes=64)
+            nc.vector.tensor_copy(
+                slot_words[g, e][:], tok_words[g][:].indirect(gather_list[:, e * (C // 16) : (e + 1) * (C // 16)])
+            )
 
-        def scatter_results(t, y):
-            placed = results.tile([P, T], F32, name="placed")
-            for e in range(E):
-                list_e = scatter_list[:, e * (C // 16) : (e + 1) * (C // 16)]
-                nc.vector.tensor_tensor(placed[:].indirect(list_e), y[t, e][:], gates[:, e * C : (e + 1) * C], MULT)
-            nc.sync.dma_start(out[t * P : (t + 1) * P, :], placed[:])
-
-        y = {}
-        for e in range(E):
-            list_e = gather_list[:, e * (C // 16) : (e + 1) * (C // 16)]
-            slot_words[1, e] = held.tile([P, C], U32, name=f"slot_words_1_{e}", align_bytes=64)
+        def gather_bytes(e):
             slot_bytes[e] = held.tile([P, C], U8, name=f"slot_bytes_{e}", align_bytes=64)
-            nc.vector.tensor_copy(slot_words[1, e][:], tok_words[1][:].indirect(list_e))
-            nc.vector.tensor_copy(slot_bytes[e][:], tok_bytes[:].indirect(list_e))
-            for t in range(N_TILES):
+            nc.vector.tensor_copy(
+                slot_bytes[e][:], tok_bytes[:].indirect(gather_list[:, e * (C // 16) : (e + 1) * (C // 16)])
+            )
+
+        grouped = {}
+
+        def interleave(g, c, n, by_scalar):
+            grouped[g, c] = held.tile([P, n, PACK], BF16, name=f"grouped_{g}_{c}", align_bytes=64)
+            by_token = raw[g][:, :, c : c + n].rearrange("p j w -> p w j")
+            nc.scalar.copy(grouped[g, c][:, :by_scalar, :], by_token[:, :by_scalar, :])
+            nc.vector.tensor_copy(grouped[g, c][:, by_scalar:, :], by_token[:, by_scalar:, :])
+
+        def quantise(g, c, n, by_scalar):
+            nc.vector.quantize_mx(
+                out=tok_words[g][:, c : c + n].bitcast(FP8X4),
+                scales=tok_bytes[first_row[g] :, c : c + n],
+                in_=grouped[g, c][:].rearrange("p w j -> p (w j)"),
+            )
+
+        interleave(*CHUNKS[0])
+        quantise(*CHUNKS[0])
+        turned = psum.tile([P, E, P], F32, name="turned")
+        for e in range(E):
+            nc.tensor.transpose(turned[:, e, :], b_rows[:, :, e], identity[:])
+        nc.scalar.copy(bias[:], turned[:, :, :N_TILES])
+        interleave(*CHUNKS[1])
+        quantise(*CHUNKS[1])
+        interleave(*CHUNKS[2])
+        gather_words(0, 0)
+        quantise(*CHUNKS[2])
+        gather_words(0, 1)
+        interleave(*CHUNKS[3])
+        quantise(*CHUNKS[3])
+
+        y = [results.tile([P, E * C], F32, name="y") for t in range(N_TILES)]
+        gather_words(1, 0)
+        gather_bytes(0)
+        gather_words(1, 1)
+        gather_bytes(1)
+        for t in range(N_TILES):
+            for e in range(E):
                 acc = psum.tile([P, T], F32, name="acc")
                 for s in range(0, C, P):
                     nc.tensor.matmul_mx(
                         out=acc[:, s : s + P],
-                        lhsT=w8[e][:, 4 * P * t : 4 * P * (t + 1)].bitcast(FP8X4),
-                        lhsT_scale=w_bytes[:, 0, e, P * t : P * (t + 1)],
+                        lhsT=w8[:, e, 4 * P * t : 4 * P * (t + 1)].bitcast(FP8X4),
+                        lhsT_scale=w_bytes[0][:, e, P * t : P * (t + 1)],
                         rhs=slot_words[0, e][:, s : s + P].bitcast(FP8X4),
                         rhs_scale=slot_bytes[e][4:, s : s + P],
                         start=True,
@@ -122,14 +146,25 @@ def tile_moe_two_lin_bias_kernel(
                     )
                     nc.tensor.matmul_mx(
                         out=acc[:, s : s + P],
-                        lhsT=w4[e][:, 2 * P * t : 2 * P * (t + 1)].bitcast(FP4X4),
-                        lhsT_scale=w_bytes[:, 1, e, P * t : P * (t + 1)],
+                        lhsT=w4[:, e, 2 * P * t : 2 * P * (t + 1)].bitcast(FP4X4),
+                        lhsT_scale=w_bytes[1][:, e, P * t : P * (t + 1)],
                         rhs=slot_words[1, e][:, s : s + P].bitcast(FP8X4),
                         rhs_scale=slot_bytes[e][:, s : s + P],
                         start=False,
                         stop=True,
                     )
-                y[t, e] = results.tile([P, C], F32, name="y")
-                nc.scalar.activation(y[t, e][:], acc[:, :C], IDENTITY, bias=bias[:, t, e : e + 1])
+                nc.scalar.activation(y[t][:, e * C : (e + 1) * C], acc[:, :C], IDENTITY, bias=bias[:, e, t : t + 1])
+
+        def place(t, window, slots):
+            nc.vector.tensor_tensor(
+                window[:].indirect(scatter_list[:, slots.start // 16 : slots.stop // 16]),
+                y[t][:, slots],
+                gates[:, slots],
+                MULT,
+            )
+
         for t in range(N_TILES):
-            scatter_results(t, y)
+            placed = results.tile([P, T], F32, name="placed")
+            for e in range(E):
+                place(t, placed, slice(e * C, (e + 1) * C))
+            nc.sync.dma_start(out[t * P : (t + 1) * P, :], placed[:])

@@ -21,7 +21,7 @@ N_TILES = N // P
 FLOPS = 2 * K * E * C * N
 BYTES = 4 * K * T + E * 512 * N + E * 256 * N + 2 * E * 16 * N + 4 * N * E + 4 * E * C + 4 * E * C + 4 * N * T
 
-CHUNKS = ((0, 0, 256, 128), (0, 256, 256, 128), (1, 0, 256, 128), (1, 256, 256, 76))
+CHUNKS = ((0, 0, 256, 80), (0, 256, 256, 80), (1, 0, 256, 256), (1, 256, 256, 80))
 
 
 def tile_moe_two_lin_bias_kernel(
@@ -30,7 +30,7 @@ def tile_moe_two_lin_bias_kernel(
     nc = tc.nc
     with (
         tc.tile_pool(name="held", bufs=1) as held,
-        tc.tile_pool(name="results", bufs=8) as results,
+        tc.tile_pool(name="results", bufs=10) as results,
         tc.psum_pool(name="psum", bufs=1) as psum,
     ):
         gather_list = held.tile([P, E * C // 16], U16, name="gather_list")
@@ -80,20 +80,13 @@ def tile_moe_two_lin_bias_kernel(
         nc.sync.dma_start(gates[:], gate[0:P, :])
         nc.sync.dma_start(scatter_list[:], dst)
 
-        slot_words = {}
-        slot_bytes = {}
+        slot_words = [held.tile([P, E * C], U32, name=f"slot_words_{g}", align_bytes=64) for g in range(PASSES)]
+        slot_bytes = held.tile([P, E * C], U8, name="slot_bytes", align_bytes=64)
         first_row = [4, 0]
 
-        def gather_words(g, e):
-            slot_words[g, e] = held.tile([P, C], U32, name=f"slot_words_{g}_{e}", align_bytes=64)
+        def gather(picked, table, start, n):
             nc.vector.tensor_copy(
-                slot_words[g, e][:], tok_words[g][:].indirect(gather_list[:, e * (C // 16) : (e + 1) * (C // 16)])
-            )
-
-        def gather_bytes(e):
-            slot_bytes[e] = held.tile([P, C], U8, name=f"slot_bytes_{e}", align_bytes=64)
-            nc.vector.tensor_copy(
-                slot_bytes[e][:], tok_bytes[:].indirect(gather_list[:, e * (C // 16) : (e + 1) * (C // 16)])
+                picked[:, start : start + n], table[:].indirect(gather_list[:, start // 16 : (start + n) // 16])
             )
 
         grouped = {}
@@ -102,7 +95,8 @@ def tile_moe_two_lin_bias_kernel(
             grouped[g, c] = held.tile([P, n, PACK], BF16, name=f"grouped_{g}_{c}", align_bytes=64)
             by_token = raw[g][:, :, c : c + n].rearrange("p j w -> p w j")
             nc.scalar.copy(grouped[g, c][:, :by_scalar, :], by_token[:, :by_scalar, :])
-            nc.vector.tensor_copy(grouped[g, c][:, by_scalar:, :], by_token[:, by_scalar:, :])
+            if by_scalar < n:
+                nc.vector.tensor_copy(grouped[g, c][:, by_scalar:, :], by_token[:, by_scalar:, :])
 
         def quantise(g, c, n, by_scalar):
             nc.vector.quantize_mx(
@@ -119,52 +113,46 @@ def tile_moe_two_lin_bias_kernel(
         nc.scalar.copy(bias[:], turned[:, :, :N_TILES])
         interleave(*CHUNKS[1])
         quantise(*CHUNKS[1])
+        for e in range(E):
+            gather(slot_words[0], tok_words[0], e * C, C)
         interleave(*CHUNKS[2])
-        gather_words(0, 0)
-        quantise(*CHUNKS[2])
-        gather_words(0, 1)
         interleave(*CHUNKS[3])
+        quantise(*CHUNKS[2])
         quantise(*CHUNKS[3])
+        for start, n in ((0, 128), (128, 384)):
+            gather(slot_words[1], tok_words[1], start, n)
+            gather(slot_bytes, tok_bytes, start, n)
 
-        y = [results.tile([P, E * C], F32, name="y") for t in range(N_TILES)]
-        gather_words(1, 0)
-        gather_bytes(0)
-        gather_words(1, 1)
-        gather_bytes(1)
-        for t in range(N_TILES):
-            for e in range(E):
-                acc = psum.tile([P, T], F32, name="acc")
-                for s in range(0, C, P):
-                    nc.tensor.matmul_mx(
-                        out=acc[:, s : s + P],
-                        lhsT=w8[:, e, 4 * P * t : 4 * P * (t + 1)].bitcast(FP8X4),
-                        lhsT_scale=w_bytes[0][:, e, P * t : P * (t + 1)],
-                        rhs=slot_words[0, e][:, s : s + P].bitcast(FP8X4),
-                        rhs_scale=slot_bytes[e][4:, s : s + P],
-                        start=True,
-                        stop=False,
-                    )
-                    nc.tensor.matmul_mx(
-                        out=acc[:, s : s + P],
-                        lhsT=w4[:, e, 2 * P * t : 2 * P * (t + 1)].bitcast(FP4X4),
-                        lhsT_scale=w_bytes[1][:, e, P * t : P * (t + 1)],
-                        rhs=slot_words[1, e][:, s : s + P].bitcast(FP8X4),
-                        rhs_scale=slot_bytes[e][:, s : s + P],
-                        start=False,
-                        stop=True,
-                    )
-                nc.scalar.activation(y[t][:, e * C : (e + 1) * C], acc[:, :C], IDENTITY, bias=bias[:, e, t : t + 1])
-
-        def place(t, window, slots):
+        placed = [held.tile([P, T], F32, name=f"placed_{t}") for t in range(N_TILES)]
+        for t, start, n in [(0, 0, 128), (1, 0, 128), (0, 128, 128), (1, 128, 128), (2, 0, 256), (3, 0, 256)] + [(t, 256, 256) for t in range(N_TILES)]:
+            e = start // C
+            acc = psum.tile([P, T], F32, name="acc")
+            for s in range(start, start + n, P):
+                nc.tensor.matmul_mx(
+                    out=acc[:, s - start : s - start + P],
+                    lhsT=w8[:, e, 4 * P * t : 4 * P * (t + 1)].bitcast(FP8X4),
+                    lhsT_scale=w_bytes[0][:, e, P * t : P * (t + 1)],
+                    rhs=slot_words[0][:, s : s + P].bitcast(FP8X4),
+                    rhs_scale=slot_bytes[4:, s : s + P],
+                    start=True,
+                    stop=False,
+                )
+                nc.tensor.matmul_mx(
+                    out=acc[:, s - start : s - start + P],
+                    lhsT=w4[:, e, 2 * P * t : 2 * P * (t + 1)].bitcast(FP4X4),
+                    lhsT_scale=w_bytes[1][:, e, P * t : P * (t + 1)],
+                    rhs=slot_words[1][:, s : s + P].bitcast(FP8X4),
+                    rhs_scale=slot_bytes[:, s : s + P],
+                    start=False,
+                    stop=True,
+                )
+            y = results.tile([P, C], F32, name="y")
+            nc.scalar.activation(y[:, :n], acc[:, :n], IDENTITY, bias=bias[:, e, t : t + 1])
             nc.vector.tensor_tensor(
-                window[:].indirect(scatter_list[:, slots.start // 16 : slots.stop // 16]),
-                y[t][:, slots],
-                gates[:, slots],
+                placed[t][:].indirect(scatter_list[:, start // 16 : (start + n) // 16]),
+                y[:, :n],
+                gates[:, start : start + n],
                 MULT,
             )
-
-        for t in range(N_TILES):
-            placed = results.tile([P, T], F32, name="placed")
-            for e in range(E):
-                place(t, placed, slice(e * C, (e + 1) * C))
-            nc.sync.dma_start(out[t * P : (t + 1) * P, :], placed[:])
+            if start + n == E * C:
+                nc.sync.dma_start(out[t * P : (t + 1) * P, :], placed[t][:])

@@ -31,7 +31,7 @@ def tile_moe_two_lin_bias_kernel(
     with (
         tc.tile_pool(name="held", bufs=1) as held,
         tc.tile_pool(name="results", bufs=10) as results,
-        tc.psum_pool(name="psum", bufs=1) as psum,
+        tc.psum_pool(name="psum", bufs=2) as psum,
     ):
         gather_list = held.tile([P, E * C // 16], U16, name="gather_list")
         scatter_list = held.tile([P, E * C // 16], U16, name="scatter_list")
@@ -65,10 +65,10 @@ def tile_moe_two_lin_bias_kernel(
         nc.scalar.dma_start(b_rows[0:N_TILES], b.rearrange("(t p) e -> t p e", p=P))
         make_identity(nc, identity[:])
         load_tokens(0, 0)
-        nc.sync.dma_start(gather_list[:], offs)
         load_scales(0, 0)
         load_scales(0, 1)
         load_tokens(0, 256)
+        nc.sync.dma_start(gather_list[:], offs)
         load_tokens(1, 0)
         load_tokens(1, 256)
         load_scales(0, 2)

import concourse.mybir as mybir
from concourse.masks import make_identity

F32 = mybir.dt.float32
BF16 = mybir.dt.bfloat16
U32 = mybir.dt.uint32
I32 = mybir.dt.int32
U16 = mybir.dt.uint16
U8 = mybir.dt.uint8
FP8X4 = mybir.dt.float8_e4m3fn_x4
FP4X4 = mybir.dt.float4_e2m1fn_x4
IDENTITY = mybir.ActivationFunctionType.Identity
MULT = mybir.AluOpType.mult

P = 128
K, T, E, C, N = 1024, 512, 2, 256, 512
PASSES = 2
PACK = 4
K_PASS = P * PACK
N_TILES = N // P
FLOPS = 2 * K * E * C * N
BYTES = 4 * K * T + E * 512 * N + E * 256 * N + 2 * E * 16 * N + 4 * N * E + 4 * E * C + 4 * E * C + 4 * N * T

CHUNKS = ((0, 0, 256, 80), (0, 256, 256, 80), (1, 0, 256, 256), (1, 256, 256, 80))


def tile_moe_two_lin_bias_kernel(
    tc, xT, w8_words, w8_scales, w4_words, w4_scales, b, gate, offs, dst, out
):
    nc = tc.nc
    with (
        tc.tile_pool(name="held", bufs=1) as held,
        tc.tile_pool(name="results", bufs=10) as results,
        tc.psum_pool(name="psum", bufs=2) as psum,
    ):
        gather_list = held.tile([P, E * C // 16], U16, name="gather_list")
        scatter_list = held.tile([P, E * C // 16], U16, name="scatter_list")
        w_bytes = [held.tile([P, E, N], U8, name=f"w_bytes_{f}", align_bytes=64) for f in range(2)]
        tok_bytes = held.tile([P, T], U8, name="tok_bytes", align_bytes=64)
        w8 = held.tile([P, E, 4 * N], U8, name="w8", align_bytes=64)
        w4 = held.tile([P, E, 2 * N], U8, name="w4", align_bytes=64)
        bias = held.tile([P, E, N_TILES], F32, name="bias")
        b_rows = held.tile([P, P, E], F32, name="b_rows")
        identity = held.tile([P, P], F32, name="identity")
        gates = held.tile([P, E * C], F32, name="gates")
        raw = [held.tile([P, PACK, T], F32, name=f"raw_{g}") for g in range(PASSES)]
        tok_words = [held.tile([P, T], U32, name=f"tok_words_{g}", align_bytes=64) for g in range(PASSES)]

        for f in range(2):
            nc.vector.memset(w_bytes[f][:].rearrange("p e n -> p (e n)").bitcast(I32), 0)
        nc.vector.memset(tok_bytes[:].bitcast(I32), 0)

        def load_tokens(g, c):
            rows = xT[g * K_PASS : (g + 1) * K_PASS, :].rearrange("(p j) w -> p j w", j=PACK)
            nc.sync.dma_start(raw[g][:, :, c : c + 256], rows[:, :, c : c + 256])

        def load_scales(f, r):
            scales = (w8_scales, w4_scales)[f]
            nc.sync.dma_start(
                w_bytes[f][32 * r : 32 * r + 4].bitcast(I32),
                scales[:, 0, 4 * r : 4 * r + 4, :].rearrange("e q n -> q e n").bitcast(I32),
            )

        nc.gpsimd.memset(b_rows[:], 0.0)
        nc.scalar.dma_start(b_rows[0:N_TILES], b.rearrange("(t p) e -> t p e", p=P))
        make_identity(nc, identity[:])
        load_tokens(0, 0)
        load_scales(0, 0)
        load_scales(0, 1)
        load_tokens(0, 256)
        nc.sync.dma_start(gather_list[:], offs)
        load_tokens(1, 0)
        load_tokens(1, 256)
        load_scales(0, 2)
        load_scales(0, 3)
        for r in range(4):
            load_scales(1, r)
        nc.sync.dma_start(w8[:].bitcast(I32), w8_words[:, 0].rearrange("e p n r -> p e (n r)").bitcast(I32))
        nc.sync.dma_start(w4[:].bitcast(I32), w4_words[:, 0].rearrange("e p n -> p e n").bitcast(I32))
        nc.sync.dma_start(gates[:], gate[0:P, :])
        nc.sync.dma_start(scatter_list[:], dst)

        slot_words = [held.tile([P, E * C], U32, name=f"slot_words_{g}", align_bytes=64) for g in range(PASSES)]
        slot_bytes = held.tile([P, E * C], U8, name="slot_bytes", align_bytes=64)
        first_row = [4, 0]

        def gather(picked, table, start, n):
            nc.vector.tensor_copy(
                picked[:, start : start + n], table[:].indirect(gather_list[:, start // 16 : (start + n) // 16])
            )

        grouped = {}

        def interleave(g, c, n, by_scalar):
            grouped[g, c] = held.tile([P, n, PACK], BF16, name=f"grouped_{g}_{c}", align_bytes=64)
            by_token = raw[g][:, :, c : c + n].rearrange("p j w -> p w j")
            nc.scalar.copy(grouped[g, c][:, :by_scalar, :], by_token[:, :by_scalar, :])
            if by_scalar < n:
                nc.vector.tensor_copy(grouped[g, c][:, by_scalar:, :], by_token[:, by_scalar:, :])

        def quantise(g, c, n, by_scalar):
            nc.vector.quantize_mx(
                out=tok_words[g][:, c : c + n].bitcast(FP8X4),
                scales=tok_bytes[first_row[g] :, c : c + n],
                in_=grouped[g, c][:].rearrange("p w j -> p (w j)"),
            )

        interleave(*CHUNKS[0])
        quantise(*CHUNKS[0])
        turned = psum.tile([P, E, P], F32, name="turned")
        for e in range(E):
            nc.tensor.transpose(turned[:, e, :], b_rows[:, :, e], identity[:])
        nc.scalar.copy(bias[:], turned[:, :, :N_TILES])
        interleave(*CHUNKS[1])
        quantise(*CHUNKS[1])
        for e in range(E):
            gather(slot_words[0], tok_words[0], e * C, C)
        interleave(*CHUNKS[2])
        interleave(*CHUNKS[3])
        quantise(*CHUNKS[2])
        quantise(*CHUNKS[3])
        for start, n in ((0, 128), (128, 384)):
            gather(slot_words[1], tok_words[1], start, n)
            gather(slot_bytes, tok_bytes, start, n)

        placed = [held.tile([P, T], F32, name=f"placed_{t}") for t in range(N_TILES)]
        for t, start, n in [(0, 0, 128), (1, 0, 128), (0, 128, 128), (1, 128, 128), (2, 0, 256), (3, 0, 256)] + [(t, 256, 256) for t in range(N_TILES)]:
            e = start // C
            acc = psum.tile([P, T], F32, name="acc")
            for s in range(start, start + n, P):
                nc.tensor.matmul_mx(
                    out=acc[:, s - start : s - start + P],
                    lhsT=w8[:, e, 4 * P * t : 4 * P * (t + 1)].bitcast(FP8X4),
                    lhsT_scale=w_bytes[0][:, e, P * t : P * (t + 1)],
                    rhs=slot_words[0][:, s : s + P].bitcast(FP8X4),
                    rhs_scale=slot_bytes[4:, s : s + P],
                    start=True,
                    stop=False,
                )
                nc.tensor.matmul_mx(
                    out=acc[:, s - start : s - start + P],
                    lhsT=w4[:, e, 2 * P * t : 2 * P * (t + 1)].bitcast(FP4X4),
                    lhsT_scale=w_bytes[1][:, e, P * t : P * (t + 1)],
                    rhs=slot_words[1][:, s : s + P].bitcast(FP8X4),
                    rhs_scale=slot_bytes[:, s : s + P],
                    start=False,
                    stop=True,
                )
            y = results.tile([P, C], F32, name="y")
            nc.scalar.activation(y[:, :n], acc[:, :n], IDENTITY, bias=bias[:, e, t : t + 1])
            nc.vector.tensor_tensor(
                placed[t][:].indirect(scatter_list[:, start // 16 : (start + n) // 16]),
                y[:, :n],
                gates[:, start : start + n],
                MULT,
            )
            if start + n == E * C:
                nc.sync.dma_start(out[t * P : (t + 1) * P, :], placed[t][:])
